import numpy as np
import ml_dtypes


def mxq(x, axis, fmt="e4m3"):
    dtype, down = {"e4m3": (ml_dtypes.float8_e4m3fn, 7), "e5m2": (ml_dtypes.float8_e5m2, 14)}[fmt]
    v = np.moveaxis(np.asarray(x, np.float32).astype(ml_dtypes.bfloat16).astype(np.float64), axis, -1)
    blocks = v.reshape(v.shape[:-1] + (-1, 32))
    amax = np.abs(blocks).max(-1, keepdims=True)
    byte = np.maximum(np.where(amax > 0, np.frexp(amax)[1] - 1 + 127, 0) - down, 1)
    scale = np.exp2(byte - 127.0)
    codes = (blocks / scale).astype(np.float32).astype(dtype).astype(np.float64)
    return np.moveaxis((codes * scale).reshape(v.shape), -1, axis)


WIDE = False


def mx_kscale(k):
    if not WIDE:
        return np.ones(k)
    levels = np.array([10, -10, 5, -5, 0])
    if k % 512:
        return np.exp2(np.random.permutation(np.resize(levels, k // 32))).repeat(32)
    a = np.empty((k // 512, 16))
    for p in range(k // 512):
        a[p, :8] = np.random.permutation(np.resize(levels, 8))
        for g in range(8):
            far = levels[np.abs(levels - a[p, g]) >= 10]
            a[p, g + 8] = far[np.random.randint(len(far))]
    return np.exp2(a.ravel()).repeat(32)


BF16 = ml_dtypes.bfloat16


def bf(x):
    return np.asarray(x, np.float32).astype(BF16)


def f64(x):
    return np.asarray(x).astype(np.float64)


H, N, G, P, D = 2, 2048, 4, 256, 512
T = G * P


def draw0():
    s, t = mx_kscale(D), mx_kscale(T)
    return {
        "q": bf(np.random.standard_normal((H, N, D)) * 1.5),
        "k_code": bf(np.random.uniform(-1.5, 1.5, (H, G, P, D)) / s),
        "k_scale": bf(np.random.uniform(0.5, 1.5, (H, G, D)) * s),
        "k_zero": bf(np.random.standard_normal((H, G, D)) * 0.3),
        "v_code": bf(np.random.uniform(-3.0, 3.0, (H, T, D)) / t[None, :, None]),
        "v_scale": bf(np.random.standard_normal((H, T)) * 2.0 * t),
    }


def grouped_scores(q, k_code, k_scale, k_zero):
    qs = q[:, None, :, :] * k_scale[:, :, None, :]
    off = np.sum(q[:, None, :, :] * k_zero[:, :, None, :], axis=-1)
    a = mxq(qs, 3, "e4m3") @ mxq(k_code, 3, "e4m3").transpose(0, 1, 3, 2)
    return (a + off[..., None]) / np.sqrt(D)


def core(q, k_code, k_scale, k_zero, v_code, v_scale):
    sc = grouped_scores(f64(q), f64(k_code), f64(k_scale), f64(k_zero))
    sc = sc.transpose(0, 2, 1, 3).reshape(H, N, T)
    e = np.exp(sc - sc.max(axis=-1, keepdims=True))
    w = e / e.sum(axis=-1, keepdims=True)
    ws = w * f64(v_scale)[:, None, :]
    return mxq(ws, 2, "e4m3") @ mxq(f64(v_code), 1, "e4m3")


def e4m3fn_bytes(y):
    return np.clip(np.asarray(y, np.float64), -448.0, 448.0).astype(np.float32).astype(ml_dtypes.float8_e4m3fn).view(np.uint8)


def e4m3fn_values(b):
    return np.asarray(b, np.uint8).view(ml_dtypes.float8_e4m3fn).astype(np.float64)


def setup_inputs():
    d = draw0()
    x0 = np.asarray(d['v_code']).astype(np.float64)
    s = (np.max(np.abs(x0), axis=(0, 2), keepdims=True) / 448.0).astype(np.float32)
    out = {}
    for k, v in d.items():
        if k == 'v_code':
            out['v_code_bytes'] = e4m3fn_bytes(x0 / s.astype(np.float64))
            out['v_code_scale'] = s
        else:
            out[k] = v
    return out


def reference(q, k_code, k_scale, k_zero, v_code_bytes, v_code_scale, v_scale):
    return core(q, k_code, k_scale, k_zero, e4m3fn_values(v_code_bytes) * v_code_scale.astype(np.float64), v_scale)

@@ -1,0 +1,500 @@
+import math
+from contextlib import ExitStack
+
+import concourse.mybir as mybir
+from concourse.masks import make_identity
+
+H, N, G, P_TOK, D = 2, 2048, 4, 256, 512
+T = G * P_TOK
+FLOPS = 4 * H * N * T * D
+
+F32 = mybir.dt.float32
+BF16 = mybir.dt.bfloat16
+U32 = mybir.dt.uint32
+U8 = mybir.dt.uint8
+FP8 = mybir.dt.float8_e4m3fn
+FP8X4 = mybir.dt.float8_e4m3fn_x4
+ALU = mybir.AluOpType
+ACT = mybir.ActivationFunctionType
+AX = mybir.AxisListType
+
+P = 128
+TILES = N // P
+CHUNK = 4
+PAIRS = TILES // 2
+STEPS = H * PAIRS
+
+PE_GROUPS = (1, 1)
+FIRST_PE = 2
+SCALE = 1.0 / math.sqrt(D)
+
+
+def tile_kivigroupedscalefoldedattention_t_kernel(
+    tc, q, k_code, k_scale, k_zero, v_code_bytes, v_code_scale, v_scale, out
+):
+    nc = tc.nc
+    with ExitStack() as ctx:
+        keep = ctx.enter_context(tc.tile_pool(name="keep", bufs=1))
+        work = ctx.enter_context(tc.tile_pool(name="work", bufs=3))
+        psum = ctx.enter_context(tc.psum_pool(name="psum", bufs=1))
+        ctx.enter_context(tc.manual_schedule())
+
+        def bank(tag, bufs=1):
+            return psum.tile([P, 512], F32, name="ps_" + tag, tag=tag, bufs=bufs)
+
+        def keep_tile(shape, dtype, name):
+            return keep.tile(shape, dtype, name=name, tag=name, align_bytes=64)
+
+        def work_tile(shape, dtype, name, bufs=3):
+            return work.tile(shape, dtype, name=name, tag=name, bufs=bufs, align_bytes=64)
+
+        ident = keep_tile([P, P], F32, "ident")
+        ident_bf = keep_tile([P, P], BF16, "ident_bf")
+        rows = keep_tile([P, D], BF16, "rows")
+        dummy = keep_tile([P, 1], F32, "dummy")
+        cols = keep_tile([P, 20, 4], BF16, "cols")
+        ks_full = [keep_tile([P, G, P, 4], BF16, "ks_full%d" % h) for h in range(H)]
+        ks_diag = [keep_tile([P, 2, 4, P], BF16, "ks_diag%d" % h) for h in range(H)]
+        k_raw = [[keep_tile([P, 4, D], BF16, "k_raw%d%d" % (h, c)) for c in range(2)] for h in range(H)]
+        k_codes = [keep_tile([P, T], U32, "k_codes%d" % h) for h in range(H)]
+        k_scales = [keep_tile([P, T], U8, "k_scales%d" % h) for h in range(H)]
+        v_bytes = [keep_tile([P, 2, 4, D], U8, "v_bytes%d" % h) for h in range(H)]
+        v_factor = keep_tile([P, 2, 4], F32, "v_factor")
+        v_codes = [keep_tile([P, 2, D], U32, "v_codes%d" % h) for h in range(H)]
+        v_scales = [keep_tile([P, 2, D], U8, "v_scales%d" % h) for h in range(H)]
+        q_raw = [keep_tile([P, CHUNK, D], BF16, "q_raw%d" % i) for i in range(2 * STEPS // CHUNK)]
+
+        q_view = q.rearrange("h (c p j) d -> (h c) p j d", p=P, j=CHUNK)
+        out_view = out.rearrange("h (c p j) d -> (h c) j p d", p=P, j=CHUNK)
+        k_view = k_code.rearrange("h g t d -> h (g t) d").rearrange("h (c p j) d -> h c p j d", p=P, j=4)
+        v_view = v_code_bytes.rearrange("h (c p j) d -> h p c j d", p=P, j=4)
+
+        nc.vector.memset(rows[:], 0.0)
+        nc.vector.memset(dummy[:], 0.0)
+        nc.scalar.activation(dummy[:], dummy[:], ACT.Exp)
+        make_identity(nc, ident[:])
+        make_identity(nc, ident_bf[:])
+        nc.sync.dma_start(out=rows[0:8, :], in_=k_scale.rearrange("h g d -> (h g) d"))
+        nc.sync.dma_start(out=rows[8:16, :], in_=k_zero.rearrange("h g d -> (h g) d"))
+        nc.sync.dma_start(out=rows[16:20, :], in_=v_scale.rearrange("h (c t) -> (h c) t", c=2))
+        nc.sync.dma_start(out=q_raw[0][:, 0:2, :], in_=q_view[0][:, 0:2, :])
+        nc.sync.dma_start(out=k_raw[0][0][:], in_=k_view[0, 0])
+        nc.sync.dma_start(out=k_raw[0][1][:], in_=k_view[0, 1])
+        nc.sync.dma_start(out=q_raw[0][:, 2:4, :], in_=q_view[0][:, 2:4, :])
+        nc.sync.dma_start(out=v_factor[:], in_=v_code_scale.rearrange("o (c p j) x -> p (o c) (j x)", p=P, j=4))
+        nc.sync.dma_start(out=v_bytes[0][:], in_=v_view[0])
+        nc.sync.dma_start(out=q_raw[1][:], in_=q_view[1])
+        nc.sync.dma_start(out=q_raw[2][:], in_=q_view[2])
+        nc.sync.dma_start(out=k_raw[1][0][:], in_=k_view[1, 0])
+        nc.sync.dma_start(out=k_raw[1][1][:], in_=k_view[1, 1])
+        nc.sync.dma_start(out=v_bytes[1][:], in_=v_view[1])
+        for i in range(3, 2 * STEPS // CHUNK):
+            nc.sync.dma_start(out=q_raw[i][:], in_=q_view[i])
+
+        q_bank, q_t, off_bank, off, qs, qs_codes, qs_scales, pe_bank = {}, {}, {}, {}, {}, {}, {}, {}
+        scores, m8, a4, m1, bias, e, s8, s2, r, en = {}, {}, {}, {}, {}, {}, {}, {}, {}, {}
+        w_bank, wg, w_codes, w_scales, o_bank = {}, {}, {}, {}, {}
+
+        def transpose_q(s):
+            q_bank[s] = bank("a", 2)
+            for i in range(2):
+                tile = 2 * s + i
+                words = q_raw[tile // CHUNK][:, tile % CHUNK, :].bitcast(F32)
+                for u in range(2):
+                    dst = (2 * i + u) * P
+                    nc.tensor.transpose(q_bank[s][:, dst : dst + P], words[:, u : D // 2 : 2], ident[:])
+
+        def copy_q(s):
+            q_t[s] = work_tile([P, 2, P, 4], BF16, "q_t", 4)
+            nc.scalar.copy(
+                q_t[s][:].rearrange("p i n x -> p (i n x)").bitcast(F32).rearrange("p (i n u) -> p i n u", i=2, u=2),
+                q_bank[s][:].rearrange("p (i u n) -> p i n u", i=2, u=2),
+            )
+
+        def matmul_off(s):
+            off_bank[s] = bank("a", 2)
+            h = s // PAIRS
+            for i in range(2):
+                for t in range(4):
+                    nc.tensor.matmul(
+                        off_bank[s][:, i * G : (i + 1) * G],
+                        lhsT=q_t[s][:, i, :, t],
+                        rhs=cols[:, 8 + h * G : 8 + (h + 1) * G, t],
+                        start=(t == 0),
+                        stop=(t == 3),
+                    )
+
+        def copy_off(s):
+            off[s] = work_tile([P, 2, G], F32, "off", 5)
+            nc.scalar.activation(
+                off[s][:].rearrange("p i g -> p (i g)"), off_bank[s][:, 0 : 2 * G], ACT.Copy, scale=SCALE
+            )
+
+        def pe_groups(s):
+            return PE_GROUPS[s % 2] if s >= FIRST_PE else 0
+
+        def new_qs(s):
+            if s not in qs:
+                qs[s] = work_tile([P, G, 2, P * 4], BF16, "qs", 3)
+            return qs[s]
+
+        def matmul_qs(s, g):
+            pe_bank[s, g] = psum.tile([P, 4, 2 * P], BF16, name="ps_b", tag="a", bufs=2)
+            for t in range(4):
+                nc.tensor.matmul(
+                    pe_bank[s, g][:, t, :],
+                    lhsT=ks_diag[s // PAIRS][:, g, t, :],
+                    rhs=q_t[s][:].rearrange("p i n x -> p (i n) x")[:, :, t],
+                    start=True,
+                    stop=True,
+                )
+
+        def copy_qs(s, g):
+            nc.scalar.copy(
+                new_qs(s)[:, g].rearrange("p i (n x) -> p i n x", x=4),
+                pe_bank[s, g][:].rearrange("p x (i n) -> p i n x", i=2),
+            )
+
+        def scale_q(s):
+            g0 = pe_groups(s)
+            shape = [P, G - g0, 2, P * 4]
+            ks = ks_full[s // PAIRS][:, g0:G].rearrange("p g n x -> p g (n x)")
+            nc.vector.tensor_tensor(
+                out=new_qs(s)[:, g0:G],
+                in0=q_t[s][:].rearrange("p i n x -> p i (n x)").unsqueeze(1).to_broadcast(shape),
+                in1=ks.unsqueeze(2).to_broadcast(shape),
+                op=ALU.mult,
+            )
+
+        def quantize_q(s):
+            qs_codes[s] = work_tile([P, G, 2, P], U32, "qs_codes")
+            qs_scales[s] = work_tile([P, G, 2, P], U8, "qs_scales")
+            nc.vector.quantize_mx(
+                out=qs_codes[s][:].rearrange("p g i n -> p (g i n)").bitcast(FP8X4),
+                scales=qs_scales[s][:].rearrange("p g i n -> p (g i n)"),
+                in_=qs[s][:].rearrange("p g i x -> p (g i x)"),
+            )
+
+        def matmul_scores(s, i):
+            h = s // PAIRS
+            scores[s, i] = [bank("sc", 4), bank("sc", 4)]
+            for g in range(G):
+                toks = slice(g * P_TOK, (g + 1) * P_TOK)
+                nc.tensor.matmul_mx(
+                    out=scores[s, i][g // 2][:, (g % 2) * P_TOK : (g % 2 + 1) * P_TOK],
+                    lhsT=qs_codes[s][:, g, i, :].bitcast(FP8X4),
+                    lhsT_scale=qs_scales[s][:, g, i, :],
+                    rhs=k_codes[h][:, toks].bitcast(FP8X4),
+                    rhs_scale=k_scales[h][:, toks],
+                    start=True,
+                    stop=True,
+                )
+
+        def group_max(s, i, c):
+            if s not in m8:
+                m8[s] = work_tile([P, 2, G], F32, "m8")
+            nc.vector.tensor_reduce(
+                out=m8[s][:, i, 2 * c : 2 * c + 2],
+                in_=scores[s, i][c][:].rearrange("p (g t) -> p g t", g=2),
+                axis=AX.X,
+                op=ALU.max,
+            )
+
+        def add_off(s, i):
+            a4[s, i] = work_tile([P, G], F32, "a4")
+            nc.vector.scalar_tensor_tensor(
+                out=a4[s, i][:], in0=m8[s][:, i, :], scalar=-SCALE, in1=off[s][:, i, :], op0=ALU.mult, op1=ALU.subtract
+            )
+
+        def row_max(s, i):
+            m1[s, i] = work_tile([P, 1], F32, "m1")
+            nc.vector.tensor_reduce(out=m1[s, i][:], in_=a4[s, i][:], axis=AX.X, op=ALU.min)
+
+        def center_off(s, i):
+            bias[s, i] = work_tile([P, G], F32, "bias")
+            nc.scalar.activation(bias[s, i][:], off[s][:, i, :], ACT.Identity, bias=m1[s, i][:, 0:1])
+
+        def exps(s, i):
+            e[s, i] = work_tile([P, 2, 4, P], F32, "e", 4)
+            if s not in s8:
+                s8[s] = work_tile([P, 2, G], F32, "s8")
+            for g in range(G):
+                c, half = g // 2, g % 2
+                nc.scalar.activation(
+                    e[s, i][:, c, :, half * 64 : (half + 1) * 64],
+                    scores[s, i][c][:, half * P_TOK : (half + 1) * P_TOK].rearrange("p (j x) -> p j x", j=4),
+                    ACT.Exp,
+                    bias=bias[s, i][:, g : g + 1],
+                    scale=SCALE,
+                    accum_out=s8[s][:, i, g : g + 1],
+                )
+
+        def row_sum(s, tiles=slice(0, 2)):
+            if s not in s2:
+                s2[s] = work_tile([P, 2], F32, "s2")
+            nc.vector.tensor_reduce(out=s2[s][:, tiles], in_=s8[s][:, tiles, :], axis=AX.X, op=ALU.add)
+
+        def recip(s, tiles=slice(0, 2)):
+            if s not in r:
+                r[s] = work_tile([P, 2], F32, "r")
+            nc.vector.reciprocal(r[s][:, tiles], s2[s][:, tiles])
+
+        def normalize(s, i, engine=nc.gpsimd):
+            en[s, i] = work_tile([P, 2, 4, P], F32, "en", 4)
+            engine.tensor_scalar(
+                out=en[s, i][:].rearrange("p c j x -> p (c j x)"),
+                in0=e[s, i][:].rearrange("p c j x -> p (c j x)"),
+                scalar1=r[s][:, i : i + 1],
+                scalar2=0.0,
+                op0=ALU.mult,
+                op1=ALU.add,
+            )
+
+        def transpose_w(s, i, c):
+            w_bank[s, i, c] = bank("w", 2)
+            for j in range(4):
+                nc.tensor.transpose(w_bank[s, i, c][:, j * P : (j + 1) * P], en[s, i][:, c, j, :], ident[:])
+
+        def weights(s, i, c):
+            if s not in wg:
+                wg[s] = work_tile([P, 2, 2, P, 4], BF16, "wg")
+            factor = cols[:, 16 + 2 * (s // PAIRS) + c, :]
+            nc.vector.tensor_tensor(
+                out=wg[s][:, i, c],
+                in0=w_bank[s, i, c][:].rearrange("p (j n) -> p n j", j=4),
+                in1=factor.unsqueeze(1).to_broadcast([P, P, 4]),
+                op=ALU.mult,
+            )
+
+        def quantize_w(s, tiles=slice(0, 2)):
+            if s not in w_codes:
+                w_codes[s] = work_tile([P, 2, 2 * P], U32, "w_codes")
+                w_scales[s] = work_tile([P, 2, 2 * P], U8, "w_scales")
+            nc.vector.quantize_mx(
+                out=w_codes[s][:, tiles].rearrange("p i x -> p (i x)").bitcast(FP8X4),
+                scales=w_scales[s][:, tiles].rearrange("p i x -> p (i x)"),
+                in_=wg[s][:, tiles].rearrange("p i c n x -> p (i c n x)"),
+            )
+
+        def matmul_out(s, i):
+            h = s // PAIRS
+            o_bank[s, i] = bank("a", 2)
+            for c in range(2):
+                queries = slice(c * P, (c + 1) * P)
+                nc.tensor.matmul_mx(
+                    out=o_bank[s, i][:],
+                    lhsT=w_codes[s][:, i, queries].bitcast(FP8X4),
+                    lhsT_scale=w_scales[s][:, i, queries],
+                    rhs=v_codes[h][:, c, :].bitcast(FP8X4),
+                    rhs_scale=v_scales[h][:, c, :],
+                    start=(c == 0),
+                    stop=(c == 1),
+                )
+
+        def store_out(s, i, copy=nc.scalar.copy):
+            o = work_tile([P, D], F32, "o_sb", 4)
+            copy(o[:], o_bank[s, i][:])
+            tile = 2 * s + i
+            nc.sync.dma_start(out=out_view[tile // CHUNK, tile % CHUNK], in_=o[:])
+
+        k_grouped, k_bank = {}, {}
+
+        def transpose_k(h, c, u, tag, bufs):
+            b = bank(tag, bufs)
+            k_bank[h, c, u] = b
+            for j in range(2):
+                words = k_raw[h][c][:, 2 * u + j, :].bitcast(F32)
+                for half in range(2):
+                    dst = (2 * j + half) * P
+                    nc.tensor.transpose(b[:, dst : dst + P], words[:, half : D // 2 : 2], ident[:])
+
+        def copy_k(h, c, u):
+            if (h, c) not in k_grouped:
+                k_grouped[h, c] = work_tile([P, 2, 4, 64, 4], BF16, "k_grouped", 2)
+            src = k_bank[h, c, u][:].rearrange("p (j w t) -> p j t w", j=2, w=2)
+            for half in range(2):
+                dst = k_grouped[h, c][:, half, 2 * u : 2 * u + 2].rearrange("p j t x -> p (j t x)").bitcast(F32)
+                nc.scalar.copy(dst.rearrange("p (j t w) -> p j t w", j=2, w=2), src[:, :, half * 64 : (half + 1) * 64, :])
+
+        def quantize_k(h, c):
+            toks = slice(c * 512, (c + 1) * 512)
+            nc.vector.quantize_mx(
+                out=k_codes[h][:, toks].bitcast(FP8X4),
+                scales=k_scales[h][:, toks],
+                in_=k_grouped[h, c][:].rearrange("p g j t x -> p (g j t x)"),
+            )
+
+        v_plain, v_grouped = {}, {}
+
+        def widen_v(h, c, j):
+            if (h, c) not in v_plain:
+                v_plain[h, c] = work_tile([P, 4, D], BF16, "v_plain", 2)
+            nc.scalar.activation(
+                v_plain[h, c][:, j, :], v_bytes[h][:, c, j, :].bitcast(FP8), ACT.Copy, scale=v_factor[:, c, j : j + 1]
+            )
+
+        def group_v(h, c, copy, part, parts):
+            if (h, c) not in v_grouped:
+                v_grouped[h, c] = work_tile([P, D, 4], BF16, "v_grouped", 2)
+            ds = slice(part * D // parts, (part + 1) * D // parts)
+            copy(v_grouped[h, c][:, ds, :], v_plain[h, c][:, :, ds].rearrange("p j d -> p d j"))
+
+        def quantize_v(h, c):
+            nc.vector.quantize_mx(
+                out=v_codes[h][:, c, :].bitcast(FP8X4),
+                scales=v_scales[h][:, c, :],
+                in_=v_grouped[h, c][:].rearrange("p d j -> p (d j)"),
+            )
+
+        def spread_ks(h):
+            nc.vector.tensor_copy(ks_full[h][:], cols[:, h * G : (h + 1) * G, :].unsqueeze(2).to_broadcast([P, G, P, 4]))
+
+        def make_diag(h):
+            for g in range(max(PE_GROUPS)):
+                for t in range(4):
+                    nc.gpsimd.tensor_scalar(
+                        out=ks_diag[h][:, g, t, :],
+                        in0=ident_bf[:],
+                        scalar1=cols[:, h * G + g, t : t + 1],
+                        scalar2=0.0,
+                        op0=ALU.mult,
+                        op1=ALU.add,
+                    )
+
+        rows_bank = bank("w", 2)
+        row_words = rows[:].bitcast(F32)
+        for u in range(2):
+            nc.tensor.transpose(rows_bank[:, u * P : (u + 1) * P], row_words[:, u : D // 2 : 2], ident[:])
+        nc.scalar.copy(
+            cols[:].rearrange("p r x -> p (r x)").bitcast(F32).rearrange("p (r u) -> p r u", u=2),
+            rows_bank[:, 0 : 2 * P].rearrange("p (u r) -> p r u", u=2)[:, 0:20],
+        )
+        spread_ks(0)
+        transpose_q(0)
+        copy_q(0)
+        scale_q(0)
+        for c in range(2):
+            for u in range(2):
+                transpose_k(0, c, u, "sc", 4)
+                copy_k(0, c, u)
+        make_diag(0)
+        for c in range(2):
+            quantize_k(0, c)
+
+        extra = {}
+
+        def at(s, slot, call, *args):
+            extra.setdefault((s, slot), []).append((call, args))
+
+        for c in range(2):
+            for j in range(4):
+                at(-1, "S", widen_v, 0, c, j)
+            at(0, "V", group_v, 0, c, nc.vector.tensor_copy, 0, 1)
+            at(c, "V", quantize_v, 0, c)
+        for c in range(2):
+            for u in range(2):
+                at(1 + c, "P", transpose_k, 1, c, u, "a", 2)
+                at(1 + c, "P", copy_k, 1, c, u)
+            at(2 + c, "V", quantize_k, 1, c)
+        at(3, "V", make_diag, 1)
+        at(4, "V", spread_ks, 1)
+        units = []
+        for c in range(2):
+            for j in range(4):
+                units.append((widen_v, 1, c, j))
+            for part in range(4):
+                units.append((group_v, 1, c, nc.scalar.copy, part, 4))
+        for n in range(len(units)):
+            at(3 + n // 3, "S%d" % (n % 3), *units[n])
+        at(6, "V", quantize_v, 1, 0)
+        at(9, "V", quantize_v, 1, 1)
+
+        def run_extra(s, slot):
+            for call, args in extra.get((s, slot), []):
+                call(*args)
+
+        def live(s):
+            return 0 <= s < STEPS
+
+        def when(s, call, *args, **named):
+            if live(s):
+                call(s, *args, **named)
+
+        for s in range(-2, STEPS):
+            when(s - 1, transpose_w, 0, 0)
+            when(s - 1, transpose_w, 0, 1)
+            when(s, group_max, 0, 0)
+            when(s, group_max, 0, 1)
+            when(s, group_max, 1, 0)
+            when(s, add_off, 0)
+            when(s, group_max, 1, 1)
+            when(s, row_max, 0)
+            when(s, center_off, 0)
+            when(s, exps, 0)
+            when(s - 2, quantize_w)
+            when(s, add_off, 1)
+            when(s - 1, weights, 0, 0)
+            when(s, row_max, 1)
+            when(s, center_off, 1)
+            when(s, exps, 1)
+            when(s - 1, weights, 0, 1)
+            when(s - 2, matmul_out, 0)
+            when(s - 2, matmul_out, 1)
+            when(s - 2, store_out, 0)
+            when(s - 2, store_out, 1)
+            when(s - 1, transpose_w, 1, 0)
+            when(s - 1, transpose_w, 1, 1)
+            when(s + 1, quantize_q)
+            when(s + 1, matmul_scores, 0)
+            when(s + 1, matmul_scores, 1)
+            if s + 2 > 0:
+                when(s + 2, scale_q)
+            when(s + 3, transpose_q)
+            run_extra(s, "S0")
+            when(s + 3, copy_q)
+            run_extra(s, "S1")
+            when(s + 2, matmul_off)
+            when(s + 2, copy_off)
+            run_extra(s, "S2")
+            if live(s + 2):
+                for g in range(pe_groups(s + 2)):
+                    matmul_qs(s + 2, g)
+                    copy_qs(s + 2, g)
+            run_extra(s, "P")
+            run_extra(s, "S")
+            run_extra(s, "V")
+            if s < STEPS - 1:
+                when(s, row_sum)
+            when(s - 1, weights, 1, 0)
+            if s < STEPS - 1:
+                when(s, recip)
+                when(s, normalize, 0)
+                when(s, normalize, 1)
+            when(s - 1, weights, 1, 1)
+
+        last = STEPS - 1
+        row_sum(last, slice(0, 1))
+        quantize_w(last - 1)
+        recip(last, slice(0, 1))
+        row_sum(last, slice(1, 2))
+        normalize(last, 0, nc.vector)
+        recip(last, slice(1, 2))
+        matmul_out(last - 1, 0)
+        store_out(last - 1, 0)
+        transpose_w(last, 0, 0)
+        transpose_w(last, 0, 1)
+        normalize(last, 1, nc.vector)
+        weights(last, 0, 0)
+        weights(last, 0, 1)
+        matmul_out(last - 1, 1)
+        store_out(last - 1, 1)
+        transpose_w(last, 1, 0)
+        transpose_w(last, 1, 1)
+        weights(last, 1, 0)
+        quantize_w(last, slice(0, 1))
+        weights(last, 1, 1)
+        matmul_out(last, 0)
+        store_out(last, 0)
+        quantize_w(last, slice(1, 2))
+        matmul_out(last, 1)
+        store_out(last, 1, nc.vector.tensor_copy)

@@ -92,7 +92,7 @@ def tile_kivigroupedscalefoldedattention_t_kernel(
             nc.sync.dma_start(out=q_raw[i][:], in_=q_view[i])
 
         q_bank, q_t, off_bank, off, qs, qs_codes, qs_scales, pe_bank = {}, {}, {}, {}, {}, {}, {}, {}
-        scores, m8, a4, m1, bias, e, s8, s2, r, en = {}, {}, {}, {}, {}, {}, {}, {}, {}, {}
+        scores, m8, a8, m2, bias, e, s8, s2, r, en = {}, {}, {}, {}, {}, {}, {}, {}, {}, {}
         w_bank, wg, w_codes, w_scales, o_bank = {}, {}, {}, {}, {}
 
         def transpose_q(s):
@@ -200,19 +200,19 @@ def tile_kivigroupedscalefoldedattention_t_kernel(
                 op=ALU.max,
             )
 
-        def add_off(s, i):
-            a4[s, i] = work_tile([P, G], F32, "a4")
+        def add_off(s):
+            a8[s] = work_tile([P, 2, G], F32, "a8")
             nc.vector.scalar_tensor_tensor(
-                out=a4[s, i][:], in0=m8[s][:, i, :], scalar=-SCALE, in1=off[s][:, i, :], op0=ALU.mult, op1=ALU.subtract
+                out=a8[s][:], in0=m8[s][:], scalar=-SCALE, in1=off[s][:], op0=ALU.mult, op1=ALU.subtract
             )
 
-        def row_max(s, i):
-            m1[s, i] = work_tile([P, 1], F32, "m1")
-            nc.vector.tensor_reduce(out=m1[s, i][:], in_=a4[s, i][:], axis=AX.X, op=ALU.min)
+        def row_max(s):
+            m2[s] = work_tile([P, 2], F32, "m2")
+            nc.vector.tensor_reduce(out=m2[s][:], in_=a8[s][:], axis=AX.X, op=ALU.min)
 
         def center_off(s, i):
             bias[s, i] = work_tile([P, G], F32, "bias")
-            nc.scalar.activation(bias[s, i][:], off[s][:, i, :], ACT.Identity, bias=m1[s, i][:, 0:1])
+            nc.scalar.activation(bias[s, i][:], off[s][:, i, :], ACT.Identity, bias=m2[s][:, i : i + 1])
 
         def exps(s, i):
             e[s, i] = work_tile([P, 2, 4, P], F32, "e", 4)
@@ -239,7 +239,8 @@ def tile_kivigroupedscalefoldedattention_t_kernel(
                 r[s] = work_tile([P, 2], F32, "r")
             nc.vector.reciprocal(r[s][:, tiles], s2[s][:, tiles])
 
-        def normalize(s, i, engine=nc.gpsimd):
+        def normalize(s, i):
+            engine = nc.vector if s == STEPS - 1 else nc.gpsimd
             en[s, i] = work_tile([P, 2, 4, P], F32, "en", 4)
             engine.tensor_scalar(
                 out=en[s, i][:].rearrange("p c j x -> p (c j x)"),
@@ -265,6 +266,10 @@ def tile_kivigroupedscalefoldedattention_t_kernel(
                 in1=factor.unsqueeze(1).to_broadcast([P, P, 4]),
                 op=ALU.mult,
             )
+
+        def normalize_scalar(s, i):
+            en[s, i] = work_tile([P, 2, 4, P], F32, "en", 4)
+            nc.scalar.activation(en[s, i][:], e[s, i][:], ACT.Copy, scale=r[s][:, i : i + 1])
 
         def quantize_w(s, tiles=slice(0, 2)):
             if s not in w_codes:
@@ -361,6 +366,15 @@ def tile_kivigroupedscalefoldedattention_t_kernel(
                         op1=ALU.add,
                     )
 
+        def quantize_w_tile(s, i):
+            quantize_w(s, slice(i, i + 1))
+
+        def normalize_second(s):
+            if s == STEPS - 1:
+                normalize(s, 1)
+            else:
+                normalize_scalar(s, 1)
+
         rows_bank = bank("w", 2)
         row_words = rows[:].bitcast(F32)
         for u in range(2):
@@ -377,6 +391,8 @@ def tile_kivigroupedscalefoldedattention_t_kernel(
             for u in range(2):
                 transpose_k(0, c, u, "sc", 4)
                 copy_k(0, c, u)
+        transpose_q(1)
+        copy_q(1)
         make_diag(0)
         for c in range(2):
             quantize_k(0, c)
@@ -388,16 +404,16 @@ def tile_kivigroupedscalefoldedattention_t_kernel(
 
         for c in range(2):
             for j in range(4):
-                at(-1, "S", widen_v, 0, c, j)
+                at(-1, "S0", widen_v, 0, c, j)
             at(0, "V", group_v, 0, c, nc.vector.tensor_copy, 0, 1)
-            at(c, "V", quantize_v, 0, c)
+            at(1, "V", quantize_v, 0, c)
         for c in range(2):
             for u in range(2):
                 at(1 + c, "P", transpose_k, 1, c, u, "a", 2)
                 at(1 + c, "P", copy_k, 1, c, u)
             at(2 + c, "V", quantize_k, 1, c)
         at(3, "V", make_diag, 1)
-        at(4, "V", spread_ks, 1)
+        at(3, "V", spread_ks, 1)
         units = []
         for c in range(2):
             for j in range(4):
@@ -405,7 +421,7 @@ def tile_kivigroupedscalefoldedattention_t_kernel(
             for part in range(4):
                 units.append((group_v, 1, c, nc.scalar.copy, part, 4))
         for n in range(len(units)):
-            at(3 + n // 3, "S%d" % (n % 3), *units[n])
+            at(3 + n // 3, ("S2", "S0", "S1")[n % 3], *units[n])
         at(6, "V", quantize_v, 1, 0)
         at(9, "V", quantize_v, 1, 1)
 
@@ -413,88 +429,59 @@ def tile_kivigroupedscalefoldedattention_t_kernel(
             for call, args in extra.get((s, slot), []):
                 call(*args)
 
-        def live(s):
-            return 0 <= s < STEPS
+        def skip(call, s):
+            if call in (transpose_q, copy_q):
+                return not 2 <= s < STEPS
+            return not (call == scale_q) <= s < STEPS
 
-        def when(s, call, *args, **named):
-            if live(s):
-                call(s, *args, **named)
-
-        for s in range(-2, STEPS):
-            when(s - 1, transpose_w, 0, 0)
-            when(s - 1, transpose_w, 0, 1)
-            when(s, group_max, 0, 0)
-            when(s, group_max, 0, 1)
-            when(s, group_max, 1, 0)
-            when(s, add_off, 0)
-            when(s, group_max, 1, 1)
-            when(s, row_max, 0)
-            when(s, center_off, 0)
-            when(s, exps, 0)
-            when(s - 2, quantize_w)
-            when(s, add_off, 1)
-            when(s - 1, weights, 0, 0)
-            when(s, row_max, 1)
-            when(s, center_off, 1)
-            when(s, exps, 1)
-            when(s - 1, weights, 0, 1)
-            when(s - 2, matmul_out, 0)
-            when(s - 2, matmul_out, 1)
-            when(s - 2, store_out, 0)
-            when(s - 2, store_out, 1)
-            when(s - 1, transpose_w, 1, 0)
-            when(s - 1, transpose_w, 1, 1)
-            when(s + 1, quantize_q)
-            when(s + 1, matmul_scores, 0)
-            when(s + 1, matmul_scores, 1)
-            if s + 2 > 0:
-                when(s + 2, scale_q)
-            when(s + 3, transpose_q)
-            run_extra(s, "S0")
-            when(s + 3, copy_q)
-            run_extra(s, "S1")
-            when(s + 2, matmul_off)
-            when(s + 2, copy_off)
-            run_extra(s, "S2")
-            if live(s + 2):
-                for g in range(pe_groups(s + 2)):
-                    matmul_qs(s + 2, g)
-                    copy_qs(s + 2, g)
-            run_extra(s, "P")
-            run_extra(s, "S")
-            run_extra(s, "V")
-            if s < STEPS - 1:
-                when(s, row_sum)
-            when(s - 1, weights, 1, 0)
-            if s < STEPS - 1:
-                when(s, recip)
-                when(s, normalize, 0)
-                when(s, normalize, 1)
-            when(s - 1, weights, 1, 1)
-
-        last = STEPS - 1
-        row_sum(last, slice(0, 1))
-        quantize_w(last - 1)
-        recip(last, slice(0, 1))
-        row_sum(last, slice(1, 2))
-        normalize(last, 0, nc.vector)
-        recip(last, slice(1, 2))
-        matmul_out(last - 1, 0)
-        store_out(last - 1, 0)
-        transpose_w(last, 0, 0)
-        transpose_w(last, 0, 1)
-        normalize(last, 1, nc.vector)
-        weights(last, 0, 0)
-        weights(last, 0, 1)
-        matmul_out(last - 1, 1)
-        store_out(last - 1, 1)
-        transpose_w(last, 1, 0)
-        transpose_w(last, 1, 1)
-        weights(last, 1, 0)
-        quantize_w(last, slice(0, 1))
-        weights(last, 1, 1)
-        matmul_out(last, 0)
-        store_out(last, 0)
-        quantize_w(last, slice(1, 2))
-        matmul_out(last, 1)
-        store_out(last, 1, nc.vector.tensor_copy)
+        order = [
+            (weights, 2, 1, 0),
+            (transpose_q, -2),
+            (group_max, 0, 0, 0),
+            (transpose_w, 1, 0, 1),
+            (transpose_w, 1, 0, 0),
+            (copy_q, -2),
+            (run_extra, None, "S2"),
+            (group_max, 0, 1, 1),
+            (group_max, 0, 1, 0),
+            (quantize_w_tile, 2, 1),
+            (add_off, 0),
+            (quantize_w_tile, 2, 0),
+            (row_max, 0),
+            (matmul_off, -2),
+            (matmul_out, 2, 0),
+            (normalize_second, 1),
+            (quantize_q, -1),
+            (weights, 1, 0, 1),
+            (weights, 1, 0, 0),
+            (center_off, 0, 0),
+            (center_off, 0, 1),
+            (scale_q, -2),
+            (run_extra, None, "V"),
+            (exps, 0, 0),
+            (transpose_w, 1, 1, 1),
+            (copy_off, -2),
+            (transpose_w, 1, 1, 0),
+            (weights, 1, 1, 1),
+            (matmul_scores, -1, 0),
+            (matmul_qs, -2, 0),
+            (exps, 0, 1),
+            (row_sum, 0),
+            (matmul_scores, -1, 1),
+            (store_out, 2, 0),
+            (run_extra, None, "S0"),
+            (group_max, -1, 0, 1),
+            (matmul_out, 2, 1),
+            (recip, 0),
+            (normalize, 0, 0),
+            (copy_qs, -2, 0),
+            (store_out, 2, 1),
+            (run_extra, None, "S1"),
+            (run_extra, None, "P"),
+        ]
+        for s in range(-2, STEPS + 2):
+            for call, lag, *args in order:
+                if lag is None:
+                    call(s, *args)
+                elif not skip(call, s - lag) and not (call in (matmul_qs, copy_qs) and args[0] >= pe_groups(s - lag)):
+                    call(s - lag, *args)

import math
from contextlib import ExitStack

import concourse.mybir as mybir
from concourse.masks import make_identity

H, N, G, P_TOK, D = 2, 2048, 4, 256, 512
T = G * P_TOK
FLOPS = 4 * H * N * T * D

F32 = mybir.dt.float32
BF16 = mybir.dt.bfloat16
U32 = mybir.dt.uint32
U8 = mybir.dt.uint8
FP8 = mybir.dt.float8_e4m3fn
FP8X4 = mybir.dt.float8_e4m3fn_x4
ALU = mybir.AluOpType
ACT = mybir.ActivationFunctionType
AX = mybir.AxisListType

P = 128
TILES = N // P
CHUNK = 4
PAIRS = TILES // 2
STEPS = H * PAIRS

PE_GROUPS = (1, 1)
FIRST_PE = 2
SCALE = 1.0 / math.sqrt(D)


def tile_kivigroupedscalefoldedattention_t_kernel(
    tc, q, k_code, k_scale, k_zero, v_code_bytes, v_code_scale, v_scale, out
):
    nc = tc.nc
    with ExitStack() as ctx:
        keep = ctx.enter_context(tc.tile_pool(name="keep", bufs=1))
        work = ctx.enter_context(tc.tile_pool(name="work", bufs=3))
        psum = ctx.enter_context(tc.psum_pool(name="psum", bufs=1))
        ctx.enter_context(tc.manual_schedule())

        def bank(tag, bufs=1):
            return psum.tile([P, 512], F32, name="ps_" + tag, tag=tag, bufs=bufs)

        def keep_tile(shape, dtype, name):
            return keep.tile(shape, dtype, name=name, tag=name, align_bytes=64)

        def work_tile(shape, dtype, name, bufs=3):
            return work.tile(shape, dtype, name=name, tag=name, bufs=bufs, align_bytes=64)

        ident = keep_tile([P, P], F32, "ident")
        ident_bf = keep_tile([P, P], BF16, "ident_bf")
        rows = keep_tile([P, D], BF16, "rows")
        dummy = keep_tile([P, 1], F32, "dummy")
        cols = keep_tile([P, 20, 4], BF16, "cols")
        ks_full = [keep_tile([P, G, P, 4], BF16, "ks_full%d" % h) for h in range(H)]
        ks_diag = [keep_tile([P, 2, 4, P], BF16, "ks_diag%d" % h) for h in range(H)]
        k_raw = [[keep_tile([P, 4, D], BF16, "k_raw%d%d" % (h, c)) for c in range(2)] for h in range(H)]
        k_codes = [keep_tile([P, T], U32, "k_codes%d" % h) for h in range(H)]
        k_scales = [keep_tile([P, T], U8, "k_scales%d" % h) for h in range(H)]
        v_bytes = [keep_tile([P, 2, 4, D], U8, "v_bytes%d" % h) for h in range(H)]
        v_factor = keep_tile([P, 2, 4], F32, "v_factor")
        v_codes = [keep_tile([P, 2, D], U32, "v_codes%d" % h) for h in range(H)]
        v_scales = [keep_tile([P, 2, D], U8, "v_scales%d" % h) for h in range(H)]
        q_raw = [keep_tile([P, CHUNK, D], BF16, "q_raw%d" % i) for i in range(2 * STEPS // CHUNK)]

        q_view = q.rearrange("h (c p j) d -> (h c) p j d", p=P, j=CHUNK)
        out_view = out.rearrange("h (c p j) d -> (h c) j p d", p=P, j=CHUNK)
        k_view = k_code.rearrange("h g t d -> h (g t) d").rearrange("h (c p j) d -> h c p j d", p=P, j=4)
        v_view = v_code_bytes.rearrange("h (c p j) d -> h p c j d", p=P, j=4)

        nc.vector.memset(rows[:], 0.0)
        nc.vector.memset(dummy[:], 0.0)
        nc.scalar.activation(dummy[:], dummy[:], ACT.Exp)
        make_identity(nc, ident[:])
        make_identity(nc, ident_bf[:])
        nc.sync.dma_start(out=rows[0:8, :], in_=k_scale.rearrange("h g d -> (h g) d"))
        nc.sync.dma_start(out=rows[8:16, :], in_=k_zero.rearrange("h g d -> (h g) d"))
        nc.sync.dma_start(out=rows[16:20, :], in_=v_scale.rearrange("h (c t) -> (h c) t", c=2))
        nc.sync.dma_start(out=q_raw[0][:, 0:2, :], in_=q_view[0][:, 0:2, :])
        nc.sync.dma_start(out=k_raw[0][0][:], in_=k_view[0, 0])
        nc.sync.dma_start(out=k_raw[0][1][:], in_=k_view[0, 1])
        nc.sync.dma_start(out=q_raw[0][:, 2:4, :], in_=q_view[0][:, 2:4, :])
        nc.sync.dma_start(out=v_factor[:], in_=v_code_scale.rearrange("o (c p j) x -> p (o c) (j x)", p=P, j=4))
        nc.sync.dma_start(out=v_bytes[0][:], in_=v_view[0])
        nc.sync.dma_start(out=q_raw[1][:], in_=q_view[1])
        nc.sync.dma_start(out=q_raw[2][:], in_=q_view[2])
        nc.sync.dma_start(out=k_raw[1][0][:], in_=k_view[1, 0])
        nc.sync.dma_start(out=k_raw[1][1][:], in_=k_view[1, 1])
        nc.sync.dma_start(out=v_bytes[1][:], in_=v_view[1])
        for i in range(3, 2 * STEPS // CHUNK):
            nc.sync.dma_start(out=q_raw[i][:], in_=q_view[i])

        q_bank, q_t, off_bank, off, qs, qs_codes, qs_scales, pe_bank = {}, {}, {}, {}, {}, {}, {}, {}
        scores, m8, a8, m2, bias, e, s8, s2, r, en = {}, {}, {}, {}, {}, {}, {}, {}, {}, {}
        w_bank, wg, w_codes, w_scales, o_bank = {}, {}, {}, {}, {}

        def transpose_q(s):
            q_bank[s] = bank("a", 2)
            for i in range(2):
                tile = 2 * s + i
                words = q_raw[tile // CHUNK][:, tile % CHUNK, :].bitcast(F32)
                for u in range(2):
                    dst = (2 * i + u) * P
                    nc.tensor.transpose(q_bank[s][:, dst : dst + P], words[:, u : D // 2 : 2], ident[:])

        def copy_q(s):
            q_t[s] = work_tile([P, 2, P, 4], BF16, "q_t", 4)
            nc.scalar.copy(
                q_t[s][:].rearrange("p i n x -> p (i n x)").bitcast(F32).rearrange("p (i n u) -> p i n u", i=2, u=2),
                q_bank[s][:].rearrange("p (i u n) -> p i n u", i=2, u=2),
            )

        def matmul_off(s):
            off_bank[s] = bank("a", 2)
            h = s // PAIRS
            for i in range(2):
                for t in range(4):
                    nc.tensor.matmul(
                        off_bank[s][:, i * G : (i + 1) * G],
                        lhsT=q_t[s][:, i, :, t],
                        rhs=cols[:, 8 + h * G : 8 + (h + 1) * G, t],
                        start=(t == 0),
                        stop=(t == 3),
                    )

        def copy_off(s):
            off[s] = work_tile([P, 2, G], F32, "off", 5)
            nc.scalar.activation(
                off[s][:].rearrange("p i g -> p (i g)"), off_bank[s][:, 0 : 2 * G], ACT.Copy, scale=SCALE
            )

        def pe_groups(s):
            return PE_GROUPS[s % 2] if s >= FIRST_PE else 0

        def new_qs(s):
            if s not in qs:
                qs[s] = work_tile([P, G, 2, P * 4], BF16, "qs", 3)
            return qs[s]

        def matmul_qs(s, g):
            pe_bank[s, g] = psum.tile([P, 4, 2 * P], BF16, name="ps_b", tag="a", bufs=2)
            for t in range(4):
                nc.tensor.matmul(
                    pe_bank[s, g][:, t, :],
                    lhsT=ks_diag[s // PAIRS][:, g, t, :],
                    rhs=q_t[s][:].rearrange("p i n x -> p (i n) x")[:, :, t],
                    start=True,
                    stop=True,
                )

        def copy_qs(s, g):
            nc.scalar.copy(
                new_qs(s)[:, g].rearrange("p i (n x) -> p i n x", x=4),
                pe_bank[s, g][:].rearrange("p x (i n) -> p i n x", i=2),
            )

        def scale_q(s):
            g0 = pe_groups(s)
            shape = [P, G - g0, 2, P * 4]
            ks = ks_full[s // PAIRS][:, g0:G].rearrange("p g n x -> p g (n x)")
            nc.vector.tensor_tensor(
                out=new_qs(s)[:, g0:G],
                in0=q_t[s][:].rearrange("p i n x -> p i (n x)").unsqueeze(1).to_broadcast(shape),
                in1=ks.unsqueeze(2).to_broadcast(shape),
                op=ALU.mult,
            )

        def quantize_q(s):
            qs_codes[s] = work_tile([P, G, 2, P], U32, "qs_codes")
            qs_scales[s] = work_tile([P, G, 2, P], U8, "qs_scales")
            nc.vector.quantize_mx(
                out=qs_codes[s][:].rearrange("p g i n -> p (g i n)").bitcast(FP8X4),
                scales=qs_scales[s][:].rearrange("p g i n -> p (g i n)"),
                in_=qs[s][:].rearrange("p g i x -> p (g i x)"),
            )

        def matmul_scores(s, i):
            h = s // PAIRS
            scores[s, i] = [bank("sc", 4), bank("sc", 4)]
            for g in range(G):
                toks = slice(g * P_TOK, (g + 1) * P_TOK)
                nc.tensor.matmul_mx(
                    out=scores[s, i][g // 2][:, (g % 2) * P_TOK : (g % 2 + 1) * P_TOK],
                    lhsT=qs_codes[s][:, g, i, :].bitcast(FP8X4),
                    lhsT_scale=qs_scales[s][:, g, i, :],
                    rhs=k_codes[h][:, toks].bitcast(FP8X4),
                    rhs_scale=k_scales[h][:, toks],
                    start=True,
                    stop=True,
                )

        def group_max(s, i, c):
            if s not in m8:
                m8[s] = work_tile([P, 2, G], F32, "m8")
            nc.vector.tensor_reduce(
                out=m8[s][:, i, 2 * c : 2 * c + 2],
                in_=scores[s, i][c][:].rearrange("p (g t) -> p g t", g=2),
                axis=AX.X,
                op=ALU.max,
            )

        def add_off(s):
            a8[s] = work_tile([P, 2, G], F32, "a8")
            nc.vector.scalar_tensor_tensor(
                out=a8[s][:], in0=m8[s][:], scalar=-SCALE, in1=off[s][:], op0=ALU.mult, op1=ALU.subtract
            )

        def row_max(s):
            m2[s] = work_tile([P, 2], F32, "m2")
            nc.vector.tensor_reduce(out=m2[s][:], in_=a8[s][:], axis=AX.X, op=ALU.min)

        def center_off(s, i):
            bias[s, i] = work_tile([P, G], F32, "bias")
            nc.scalar.activation(bias[s, i][:], off[s][:, i, :], ACT.Identity, bias=m2[s][:, i : i + 1])

        def exps(s, i):
            e[s, i] = work_tile([P, 2, 4, P], F32, "e", 4)
            if s not in s8:
                s8[s] = work_tile([P, 2, G], F32, "s8")
            for g in range(G):
                c, half = g // 2, g % 2
                nc.scalar.activation(
                    e[s, i][:, c, :, half * 64 : (half + 1) * 64],
                    scores[s, i][c][:, half * P_TOK : (half + 1) * P_TOK].rearrange("p (j x) -> p j x", j=4),
                    ACT.Exp,
                    bias=bias[s, i][:, g : g + 1],
                    scale=SCALE,
                    accum_out=s8[s][:, i, g : g + 1],
                )

        def row_sum(s, tiles=slice(0, 2)):
            if s not in s2:
                s2[s] = work_tile([P, 2], F32, "s2")
            nc.vector.tensor_reduce(out=s2[s][:, tiles], in_=s8[s][:, tiles, :], axis=AX.X, op=ALU.add)

        def recip(s, tiles=slice(0, 2)):
            if s not in r:
                r[s] = work_tile([P, 2], F32, "r")
            nc.vector.reciprocal(r[s][:, tiles], s2[s][:, tiles])

        def normalize(s, i):
            engine = nc.vector if s == STEPS - 1 else nc.gpsimd
            en[s, i] = work_tile([P, 2, 4, P], F32, "en", 4)
            engine.tensor_scalar(
                out=en[s, i][:].rearrange("p c j x -> p (c j x)"),
                in0=e[s, i][:].rearrange("p c j x -> p (c j x)"),
                scalar1=r[s][:, i : i + 1],
                scalar2=0.0,
                op0=ALU.mult,
                op1=ALU.add,
            )

        def transpose_w(s, i, c):
            w_bank[s, i, c] = bank("w", 2)
            for j in range(4):
                nc.tensor.transpose(w_bank[s, i, c][:, j * P : (j + 1) * P], en[s, i][:, c, j, :], ident[:])

        def weights(s, i, c):
            if s not in wg:
                wg[s] = work_tile([P, 2, 2, P, 4], BF16, "wg")
            factor = cols[:, 16 + 2 * (s // PAIRS) + c, :]
            nc.vector.tensor_tensor(
                out=wg[s][:, i, c],
                in0=w_bank[s, i, c][:].rearrange("p (j n) -> p n j", j=4),
                in1=factor.unsqueeze(1).to_broadcast([P, P, 4]),
                op=ALU.mult,
            )

        def normalize_scalar(s, i):
            en[s, i] = work_tile([P, 2, 4, P], F32, "en", 4)
            nc.scalar.activation(en[s, i][:], e[s, i][:], ACT.Copy, scale=r[s][:, i : i + 1])

        def quantize_w(s, tiles=slice(0, 2)):
            if s not in w_codes:
                w_codes[s] = work_tile([P, 2, 2 * P], U32, "w_codes")
                w_scales[s] = work_tile([P, 2, 2 * P], U8, "w_scales")
            nc.vector.quantize_mx(
                out=w_codes[s][:, tiles].rearrange("p i x -> p (i x)").bitcast(FP8X4),
                scales=w_scales[s][:, tiles].rearrange("p i x -> p (i x)"),
                in_=wg[s][:, tiles].rearrange("p i c n x -> p (i c n x)"),
            )

        def matmul_out(s, i):
            h = s // PAIRS
            o_bank[s, i] = bank("a", 2)
            for c in range(2):
                queries = slice(c * P, (c + 1) * P)
                nc.tensor.matmul_mx(
                    out=o_bank[s, i][:],
                    lhsT=w_codes[s][:, i, queries].bitcast(FP8X4),
                    lhsT_scale=w_scales[s][:, i, queries],
                    rhs=v_codes[h][:, c, :].bitcast(FP8X4),
                    rhs_scale=v_scales[h][:, c, :],
                    start=(c == 0),
                    stop=(c == 1),
                )

        def store_out(s, i, copy=nc.scalar.copy):
            o = work_tile([P, D], F32, "o_sb", 4)
            copy(o[:], o_bank[s, i][:])
            tile = 2 * s + i
            nc.sync.dma_start(out=out_view[tile // CHUNK, tile % CHUNK], in_=o[:])

        k_grouped, k_bank = {}, {}

        def transpose_k(h, c, u, tag, bufs):
            b = bank(tag, bufs)
            k_bank[h, c, u] = b
            for j in range(2):
                words = k_raw[h][c][:, 2 * u + j, :].bitcast(F32)
                for half in range(2):
                    dst = (2 * j + half) * P
                    nc.tensor.transpose(b[:, dst : dst + P], words[:, half : D // 2 : 2], ident[:])

        def copy_k(h, c, u):
            if (h, c) not in k_grouped:
                k_grouped[h, c] = work_tile([P, 2, 4, 64, 4], BF16, "k_grouped", 2)
            src = k_bank[h, c, u][:].rearrange("p (j w t) -> p j t w", j=2, w=2)
            for half in range(2):
                dst = k_grouped[h, c][:, half, 2 * u : 2 * u + 2].rearrange("p j t x -> p (j t x)").bitcast(F32)
                nc.scalar.copy(dst.rearrange("p (j t w) -> p j t w", j=2, w=2), src[:, :, half * 64 : (half + 1) * 64, :])

        def quantize_k(h, c):
            toks = slice(c * 512, (c + 1) * 512)
            nc.vector.quantize_mx(
                out=k_codes[h][:, toks].bitcast(FP8X4),
                scales=k_scales[h][:, toks],
                in_=k_grouped[h, c][:].rearrange("p g j t x -> p (g j t x)"),
            )

        v_plain, v_grouped = {}, {}

        def widen_v(h, c, j):
            if (h, c) not in v_plain:
                v_plain[h, c] = work_tile([P, 4, D], BF16, "v_plain", 2)
            nc.scalar.activation(
                v_plain[h, c][:, j, :], v_bytes[h][:, c, j, :].bitcast(FP8), ACT.Copy, scale=v_factor[:, c, j : j + 1]
            )

        def group_v(h, c, copy, part, parts):
            if (h, c) not in v_grouped:
                v_grouped[h, c] = work_tile([P, D, 4], BF16, "v_grouped", 2)
            ds = slice(part * D // parts, (part + 1) * D // parts)
            copy(v_grouped[h, c][:, ds, :], v_plain[h, c][:, :, ds].rearrange("p j d -> p d j"))

        def quantize_v(h, c):
            nc.vector.quantize_mx(
                out=v_codes[h][:, c, :].bitcast(FP8X4),
                scales=v_scales[h][:, c, :],
                in_=v_grouped[h, c][:].rearrange("p d j -> p (d j)"),
            )

        def spread_ks(h):
            nc.vector.tensor_copy(ks_full[h][:], cols[:, h * G : (h + 1) * G, :].unsqueeze(2).to_broadcast([P, G, P, 4]))

        def make_diag(h):
            for g in range(max(PE_GROUPS)):
                for t in range(4):
                    nc.gpsimd.tensor_scalar(
                        out=ks_diag[h][:, g, t, :],
                        in0=ident_bf[:],
                        scalar1=cols[:, h * G + g, t : t + 1],
                        scalar2=0.0,
                        op0=ALU.mult,
                        op1=ALU.add,
                    )

        def quantize_w_tile(s, i):
            quantize_w(s, slice(i, i + 1))

        def normalize_second(s):
            if s == STEPS - 1:
                normalize(s, 1)
            else:
                normalize_scalar(s, 1)

        rows_bank = bank("w", 2)
        row_words = rows[:].bitcast(F32)
        for u in range(2):
            nc.tensor.transpose(rows_bank[:, u * P : (u + 1) * P], row_words[:, u : D // 2 : 2], ident[:])
        nc.scalar.copy(
            cols[:].rearrange("p r x -> p (r x)").bitcast(F32).rearrange("p (r u) -> p r u", u=2),
            rows_bank[:, 0 : 2 * P].rearrange("p (u r) -> p r u", u=2)[:, 0:20],
        )
        spread_ks(0)
        transpose_q(0)
        copy_q(0)
        scale_q(0)
        for c in range(2):
            for u in range(2):
                transpose_k(0, c, u, "sc", 4)
                copy_k(0, c, u)
        transpose_q(1)
        copy_q(1)
        make_diag(0)
        for c in range(2):
            quantize_k(0, c)

        extra = {}

        def at(s, slot, call, *args):
            extra.setdefault((s, slot), []).append((call, args))

        for c in range(2):
            for j in range(4):
                at(-1, "S0", widen_v, 0, c, j)
            at(0, "V", group_v, 0, c, nc.vector.tensor_copy, 0, 1)
            at(1, "V", quantize_v, 0, c)
        for c in range(2):
            for u in range(2):
                at(1 + c, "P", transpose_k, 1, c, u, "a", 2)
                at(1 + c, "P", copy_k, 1, c, u)
            at(2 + c, "V", quantize_k, 1, c)
        at(3, "V", make_diag, 1)
        at(3, "V", spread_ks, 1)
        units = []
        for c in range(2):
            for j in range(4):
                units.append((widen_v, 1, c, j))
            for part in range(4):
                units.append((group_v, 1, c, nc.scalar.copy, part, 4))
        for n in range(len(units)):
            at(3 + n // 3, ("S2", "S0", "S1")[n % 3], *units[n])
        at(6, "V", quantize_v, 1, 0)
        at(9, "V", quantize_v, 1, 1)

        def run_extra(s, slot):
            for call, args in extra.get((s, slot), []):
                call(*args)

        def skip(call, s):
            if call in (transpose_q, copy_q):
                return not 2 <= s < STEPS
            return not (call == scale_q) <= s < STEPS

        order = [
            (weights, 2, 1, 0),
            (transpose_q, -2),
            (group_max, 0, 0, 0),
            (transpose_w, 1, 0, 1),
            (transpose_w, 1, 0, 0),
            (copy_q, -2),
            (run_extra, None, "S2"),
            (group_max, 0, 1, 1),
            (group_max, 0, 1, 0),
            (quantize_w_tile, 2, 1),
            (add_off, 0),
            (quantize_w_tile, 2, 0),
            (row_max, 0),
            (matmul_off, -2),
            (matmul_out, 2, 0),
            (normalize_second, 1),
            (quantize_q, -1),
            (weights, 1, 0, 1),
            (weights, 1, 0, 0),
            (center_off, 0, 0),
            (center_off, 0, 1),
            (scale_q, -2),
            (run_extra, None, "V"),
            (exps, 0, 0),
            (transpose_w, 1, 1, 1),
            (copy_off, -2),
            (transpose_w, 1, 1, 0),
            (weights, 1, 1, 1),
            (matmul_scores, -1, 0),
            (matmul_qs, -2, 0),
            (exps, 0, 1),
            (row_sum, 0),
            (matmul_scores, -1, 1),
            (store_out, 2, 0),
            (run_extra, None, "S0"),
            (group_max, -1, 0, 1),
            (matmul_out, 2, 1),
            (recip, 0),
            (normalize, 0, 0),
            (copy_qs, -2, 0),
            (store_out, 2, 1),
            (run_extra, None, "S1"),
            (run_extra, None, "P"),
        ]
        for s in range(-2, STEPS + 2):
            for call, lag, *args in order:
                if lag is None:
                    call(s, *args)
                elif not skip(call, s - lag) and not (call in (matmul_qs, copy_qs) and args[0] >= pe_groups(s - lag)):
                    call(s - lag, *args)
